import numpy as np
import ml_dtypes


def mxq(x, axis, fmt="e4m3"):
    dtype, down = {"e4m3": (ml_dtypes.float8_e4m3fn, 7), "e5m2": (ml_dtypes.float8_e5m2, 14)}[fmt]
    v = np.moveaxis(np.asarray(x, np.float32).astype(ml_dtypes.bfloat16).astype(np.float64), axis, -1)
    blocks = v.reshape(v.shape[:-1] + (-1, 32))
    amax = np.abs(blocks).max(-1, keepdims=True)
    byte = np.maximum(np.where(amax > 0, np.frexp(amax)[1] - 1 + 127, 0) - down, 1)
    scale = np.exp2(byte - 127.0)
    codes = (blocks / scale).astype(np.float32).astype(dtype).astype(np.float64)
    return np.moveaxis((codes * scale).reshape(v.shape), -1, axis)


WIDE = False


def mx_kscale(k):
    if not WIDE:
        return np.ones(k)
    levels = np.array([10, -10, 5, -5, 0])
    if k % 512:
        return np.exp2(np.random.permutation(np.resize(levels, k // 32))).repeat(32)
    a = np.empty((k // 512, 16))
    for p in range(k // 512):
        a[p, :8] = np.random.permutation(np.resize(levels, 8))
        for g in range(8):
            far = levels[np.abs(levels - a[p, g]) >= 10]
            a[p, g + 8] = far[np.random.randint(len(far))]
    return np.exp2(a.ravel()).repeat(32)


def f64(x):
    return np.asarray(x).astype(np.float64)


def striped(idx):
    return np.tile(idx.reshape(-1, 16).T, (8, 1)).astype(np.uint16)


def unstriped(offs):
    return offs[:16].T.reshape(-1).astype(np.int64)


E2M1 = np.array([0.0, 0.5, 1.0, 1.5, 2.0, 3.0, 4.0, 6.0, -0.0, -0.5, -1.0, -1.5, -2.0, -3.0, -4.0, -6.0])


def pack_weight(w, fmt):
    k, n = w.shape
    w = f64(np.asarray(w, np.float32).astype(ml_dtypes.bfloat16)).reshape(k // 32, 32, n)
    amax = np.abs(w).max(1)
    if fmt == "e4m3":
        byte = np.frexp(amax)[1] - 1 + 127 - 7
    else:
        mant, ex = np.frexp(amax / 6.0)
        byte = np.where(mant > 0.5, ex, ex - 1) + 127
    byte = np.clip(np.where(amax > 0, byte, 1), 1, 254)
    scaled = (w * np.exp2(127.0 - byte)[:, None, :]).reshape(k, n).astype(np.float32)
    by_word = np.ascontiguousarray(scaled.reshape(k // 512, 128, 4, n).transpose(0, 1, 3, 2))
    if fmt == "e4m3":
        words = by_word.astype(ml_dtypes.float8_e4m3fn).view(np.uint8)
    else:
        c = by_word.astype(ml_dtypes.float4_e2m1fn).view(np.uint8) & 0xF
        words = (c[..., 0::2] | (c[..., 1::2] << 4)).reshape(k // 512, 128, 2 * n)
    return np.ascontiguousarray(words), np.ascontiguousarray(byte.astype(np.uint8).reshape(k // 512, 16, n))


def unpack_weight(words, scales, fmt):
    g, _, n = scales.shape
    words = np.ascontiguousarray(words).reshape(g, 128, n, -1)
    if fmt == "e4m3":
        vals = words.view(ml_dtypes.float8_e4m3fn).astype(np.float64)
    else:
        nib = np.empty((g, 128, n, 4), np.uint8)
        nib[..., 0::2] = words & 0xF
        nib[..., 1::2] = words >> 4
        vals = E2M1[nib]
    vals = vals * np.repeat(np.exp2(scales.astype(np.float64) - 127.0), 8, axis=1)[..., None]
    return vals.transpose(0, 1, 3, 2).reshape(g * 512, n)


def gelu(v):
    return 0.5 * v * (1.0 + np.tanh(np.sqrt(2.0 / np.pi) * (v + 0.044715 * v**3)))


def striped8(idx):
    return np.concatenate([v.reshape(-1, 16).T for v in idx]).astype(np.uint16)


def unstriped8(offs):
    return np.stack([offs[16 * g:16 * g + 16].T.reshape(-1) for g in range(8)]).astype(np.int64)


def heads(xT, wgt, idx8):
    k = np.arange(xT.shape[0])
    return wgt[k // 4 % 128] * xT[k[:, None], idx8[k % 512 // 64]]


K, T, S, H, N, G, P = 1024, 2048, 1024, 1024, 512, 8, 128

def setup_inputs():
    n = np.random.standard_normal
    s = mx_kscale(K)[:, None]
    u = mx_kscale(H)[:, None]
    idx8 = np.stack([np.random.permutation(T)[:S] for _ in range(G)])
    w2_words, w2_scales = pack_weight(n((H, N)) / np.sqrt(H) / u, "e2m1")
    return {
        "xT": (n((K, T)) * s).astype(np.float32),
        "wgt": np.repeat(np.random.uniform(0.5, 2.0, (G, S)), P // G, axis=0).astype(np.float32),
        "offs": striped8(idx8),
        "w1": (n((K, H)) / np.sqrt(K) / s).astype(np.float32),
        "b1": (0.3 * n(H)).astype(np.float32),
        "gain": (np.random.uniform(0.5, 1.5, H) * u[:, 0]).astype(np.float32),
        "w2_words": w2_words,
        "w2_scales": w2_scales,
        "eT": n((N, S)).astype(np.float32),
    }

def reference(xT, wgt, offs, w1, b1, gain, w2_words, w2_scales, eT):
    xg = heads(f64(xT), f64(wgt), unstriped8(offs))
    xq = mxq(xg, 0, "e4m3")
    w1q = mxq(f64(w1), 0, "e4m3")
    a = (w1q.T @ xq) + f64(b1)[:, None]
    m = f64(gain)[:, None] * np.square(np.maximum(a, 0))
    mq = mxq(m, 0, "e4m3")
    w2 = unpack_weight(w2_words, w2_scales, "e2m1")
    return f64(eT) + (w2.T @ mq)

@@ -1,0 +1,246 @@
+from contextlib import ExitStack
+
+import concourse.mybir as mybir
+
+K, T, S, H, N = 1024, 2048, 1024, 1024, 512
+FLOPS = 2 * K * H * S + 2 * H * N * S
+
+F32 = mybir.dt.float32
+BF16 = mybir.dt.bfloat16
+I32 = mybir.dt.int32
+U32 = mybir.dt.uint32
+U16 = mybir.dt.uint16
+U8 = mybir.dt.uint8
+FP8X4 = mybir.dt.float8_e4m3fn_x4
+FP4X4 = mybir.dt.float4_e2m1fn_x4
+ALU = mybir.AluOpType
+ACT = mybir.ActivationFunctionType
+
+P = 128
+PACK = 4
+KP = P * PACK
+BANK = 512
+SQRT_FLOOR = 2.0 ** -110
+
+SIGN_WIDTH = 256
+
+
+def tile_list_relation_edge_messages_kernel(tc, xT, wgt, offs, w1, b1, gain, w2_words, w2_scales, eT, out):
+    nc = tc.nc
+    with ExitStack() as ctx:
+        keep = ctx.enter_context(tc.tile_pool(name="keep", bufs=1))
+        ring = ctx.enter_context(tc.tile_pool(name="ring", bufs=2))
+        psum = ctx.enter_context(tc.psum_pool(name="psum", bufs=1))
+
+        offsets = keep.tile([P, S // 16], U16, name="offsets")
+        nc.sync.dma_start(offsets[:], offs)
+        weights = keep.tile([P, S], F32, name="weights")
+
+        x_rows = xT.rearrange("(a p i) t -> a i p t", a=2, i=PACK)
+        planes = {}
+
+        def load_x(a, i):
+            planes[a, i] = keep.tile([P, T], F32, name=f"x_{a}_{i}", tag=f"slot_{a}_{i}", align_bytes=64)
+            nc.sync.dma_start(planes[a, i][:], x_rows[a, i])
+
+        w1_rows = w1.rearrange("(a p i) (b c) -> a b p i c", a=2, i=PACK, b=2)
+        w1_raw = {}
+
+        def load_w1(a, b):
+            w1_raw[a, b] = keep.tile([P, PACK, KP], F32, name=f"w1_raw_{a}_{b}")
+            nc.sync.dma_start(w1_raw[a, b][:], w1_rows[a, b])
+
+        bias = keep.tile([P, 2, PACK], F32, name="bias")
+        gains = keep.tile([P, 2, PACK], F32, name="gains")
+        w2_codes = keep.tile([P, 2, 2 * N], U8, name="w2_codes", align_bytes=64)
+        w2_plane = keep.tile([P, 2, N], U8, name="w2_plane", align_bytes=64)
+        nc.gpsimd.memset(w2_plane[:].rearrange("p a c -> p (a c)").bitcast(I32), 0)
+
+        nc.sync.dma_start(gains[:], gain.rearrange("(b p t) -> p b t", b=2, t=PACK))
+        nc.sync.dma_start(bias[:], b1.rearrange("(b p t) -> p b t", b=2, t=PACK))
+        nc.sync.dma_start(weights[:], wgt)
+        for i in range(PACK):
+            load_x(0, i)
+        load_x(1, 0)
+        load_x(1, 1)
+        load_w1(0, 0)
+        load_x(1, 2)
+        load_w1(1, 0)
+        load_x(1, 3)
+        load_w1(0, 1)
+        load_w1(1, 1)
+        nc.sync.dma_start(w2_codes[:].bitcast(I32), w2_words.rearrange("a p c -> p a c").bitcast(I32))
+        for q in range(4):
+            nc.sync.dma_start(
+                w2_plane[32 * q : 32 * q + 4, :, :].bitcast(I32),
+                w2_scales[:, 4 * q : 4 * q + 4, :].rearrange("a r c -> r a c").bitcast(I32),
+            )
+        e_rows = eT.rearrange("(n p) j -> p n j", p=P)
+        out_rows = out.rearrange("(n p) j -> p n j", p=P)
+        old = []
+        for h in range(2):
+            old.append(keep.tile([P, N // P, BANK], F32, name=f"old_{h}", tag=f"slot_0_{h}", align_bytes=64))
+            nc.sync.dma_start(old[h][:], e_rows[:, :, h * BANK : (h + 1) * BANK])
+
+        flat_gain = gains[:].rearrange("p b t -> p (b t)")
+        size = keep.tile([P, 8], F32, name="size")
+        nc.vector.scalar_tensor_tensor(size[:], flat_gain, -1.0, flat_gain, ALU.mult, ALU.max)
+        floored = keep.tile([P, 8], F32, name="floored")
+        nc.vector.tensor_scalar_max(floored[:], size[:], SQRT_FLOOR)
+        guess = keep.tile([P, 8], F32, name="guess")
+        nc.scalar.activation(guess[:], floored[:], ACT.Sqrt)
+        inverse = keep.tile([P, 8], F32, name="inverse")
+        nc.vector.reciprocal(inverse[:], guess[:])
+        quotient = keep.tile([P, 8], F32, name="quotient")
+        nc.vector.tensor_tensor(quotient[:], size[:], inverse[:], ALU.mult)
+        twice = keep.tile([P, 8], F32, name="twice")
+        nc.vector.tensor_tensor(twice[:], quotient[:], guess[:], ALU.add)
+        root = keep.tile([P, 8], F32, name="root")
+        nc.vector.tensor_scalar_mul(root[:], twice[:], 0.5)
+        root_bias = keep.tile([P, 8], F32, name="root_bias")
+        nc.vector.tensor_tensor(root_bias[:], root[:], bias[:].rearrange("p b t -> p (b t)"), ALU.mult)
+        signs = []
+        for b in range(2):
+            signs.append(keep.tile([P, SIGN_WIDTH, PACK], BF16, name=f"signs_{b}"))
+            nc.scalar.activation(signs[b][:], gains[:, b, :].unsqueeze(1).to_broadcast([P, SIGN_WIDTH, PACK]), ACT.Sign)
+
+        x_codes = {}
+        x_scales = [keep.tile([P, S], U8, name=f"x_scales_{a}", align_bytes=64) for a in range(2)]
+        m_codes = [keep.tile([P, S], U32, name=f"m_codes_{b}", align_bytes=64) for b in range(2)]
+        m_scales = [keep.tile([P, S], U8, name=f"m_scales_{b}", align_bytes=64) for b in range(2)]
+        w1_codes, w1_scales = {}, {}
+
+        picked = {}
+
+        def gather(a, i, j0, j1):
+            width = j1 - j0
+            if i == 0:
+                picked[a, j0] = keep.tile([P, PACK * width], F32, name=f"picked_{a}_{j0}", align_bytes=64)
+            nc.vector.tensor_tensor(
+                picked[a, j0][:, i * width : (i + 1) * width],
+                planes[a, i][:].indirect(offsets[:, j0 // 16 : j1 // 16]),
+                weights[:, j0:j1],
+                ALU.mult,
+            )
+
+        def x_words(a, j0, j1):
+            h, c0 = divmod(j0, BANK)
+            return x_codes[a, h][:, c0 : c0 + j1 - j0].bitcast(FP8X4)
+
+        def weave(a, j0, j1, copy, woven=None):
+            if woven is None:
+                woven = ring.tile([P, (j1 - j0) * PACK], BF16, name="woven", tag="woven", bufs=2, align_bytes=64)[:]
+            copy(
+                woven.rearrange("p (c e i) -> p c i e", e=4, i=PACK),
+                picked[a, j0][:].rearrange("p (i c e) -> p c i e", e=4, i=PACK),
+            )
+            nc.vector.quantize_mx(x_words(a, j0, j1), x_scales[a][:, j0:j1], woven)
+
+        def quantize_w1(a, b, copy, codes=None):
+            grouped = ring.tile([P, PACK, P, PACK], BF16, name="grouped", tag="grouped", bufs=2, align_bytes=64)
+            copy(
+                grouped[:].rearrange("p t m i -> p m i t"), w1_raw[a, b][:].rearrange("p i (m t) -> p m i t", t=PACK)
+            )
+            if codes is None:
+                codes = keep.tile([P, KP], U32, name=f"w1_codes_{a}_{b}", align_bytes=64)[:]
+            w1_codes[a, b] = codes
+            w1_scales[a, b] = keep.tile([P, KP], U8, name=f"w1_scales_{a}_{b}", align_bytes=64)
+            nc.vector.quantize_mx(
+                codes.bitcast(FP8X4), w1_scales[a, b][:], grouped[:].rearrange("p t m i -> p (t m i)")
+            )
+
+        def message(b, j0, j1, square_on_vector=False):
+            width = j1 - j0
+            rect = ring.tile([P, PACK, width], F32, name="rect", tag="rect", bufs=3)
+            for t in range(PACK):
+                acc = psum.tile([P, BANK], F32, name="acc", tag="acc", bufs=5)
+                for a in range(2):
+                    nc.tensor.matmul_mx(
+                        acc[:, :width],
+                        lhsT=w1_codes[a, b][:, t * P : (t + 1) * P].bitcast(FP8X4),
+                        lhsT_scale=w1_scales[a, b][:, t * P : (t + 1) * P],
+                        rhs=x_words(a, j0, j1),
+                        rhs_scale=x_scales[a][:, j0:j1],
+                        start=(a == 0),
+                        stop=(a == 1),
+                    )
+                col = PACK * b + t
+                nc.scalar.activation(
+                    rect[:, t, :], acc[:, :width], ACT.Relu, bias=root_bias[:, col : col + 1], scale=root[:, col : col + 1]
+                )
+            squared = ring.tile([P, width, PACK], BF16, name="squared", tag="squared", bufs=3, align_bytes=64)
+            woven_out = squared[:].rearrange("p (c e) t -> p c t e", e=4)
+            woven_in = rect[:].rearrange("p t (c e) -> p c t e", e=4)
+            if square_on_vector:
+                nc.vector.tensor_tensor(woven_out, woven_in, woven_in, ALU.mult)
+            else:
+                nc.scalar.activation(woven_out, woven_in, ACT.Square)
+            signed = ring.tile([P, width * PACK], BF16, name="signed", tag="signed", bufs=2, align_bytes=64)
+            run = min(width, SIGN_WIDTH)
+            nc.vector.tensor_tensor(
+                signed[:].rearrange("p (r e) -> p r e", e=run * PACK),
+                squared[:].rearrange("p (r j) t -> p r (j t)", j=run),
+                signs[b][:, :run, :].rearrange("p j t -> p (j t)").unsqueeze(1).to_broadcast([P, width // run, run * PACK]),
+                ALU.mult,
+            )
+            nc.vector.quantize_mx(m_codes[b][:, j0:j1].bitcast(FP8X4), m_scales[b][:, j0:j1], signed[:])
+
+        def update(j0, j1):
+            width = j1 - j0
+            step = BANK if width == BANK else P
+            per_bank = BANK // width
+            h, e0 = divmod(j0, BANK)
+            for n0 in range(0, N // P, per_bank):
+                total = psum.tile([P, per_bank, width], F32, name="total", tag="total", bufs=3)
+                for n in range(n0, n0 + per_bank):
+                    for c0 in range(0, width, step):
+                        for b in range(2):
+                            nc.tensor.matmul_mx(
+                                total[:, n - n0, c0 : c0 + step],
+                                lhsT=w2_codes[:, b, 2 * P * n : 2 * P * (n + 1)].bitcast(FP4X4),
+                                lhsT_scale=w2_plane[:, b, P * n : P * (n + 1)],
+                                rhs=m_codes[b][:, j0 + c0 : j0 + c0 + step].bitcast(FP8X4),
+                                rhs_scale=m_scales[b][:, j0 + c0 : j0 + c0 + step],
+                                start=(b == 0),
+                                stop=(b == 1),
+                            )
+                result = old[h][:, n0 : n0 + per_bank, e0 : e0 + width]
+                nc.vector.tensor_tensor(result, total[:], result, ALU.add)
+                nc.sync.dma_start(out_rows[:, n0 : n0 + per_bank, j0:j1], result)
+
+        on_scalar, on_vector = nc.scalar.copy, nc.vector.tensor_copy
+        for i in range(PACK):
+            for j0 in (0, BANK):
+                gather(0, i, j0, j0 + BANK)
+        late_chunks = ((0, 256), (256, 512), (512, 1024))
+        for i in range(PACK - 1):
+            for j0, j1 in late_chunks:
+                gather(1, i, j0, j1)
+        for a in range(2):
+            for h in range(2):
+                x_codes[a, h] = keep.tile([P, BANK], U32, name=f"x_codes_{a}_{h}", align_bytes=64)[:]
+        weave(0, 0, BANK, on_scalar)
+        weave(0, BANK, S, on_scalar)
+        quantize_w1(0, 0, on_scalar)
+        quantize_w1(1, 0, on_scalar)
+        gather(1, 3, 0, 256)
+        weave(1, 0, 256, on_scalar, picked[1, 512][:, 3 * BANK :].bitcast(BF16))
+        gather(1, 3, 256, 512)
+        weave(1, 256, 512, on_scalar)
+        quantize_w1(0, 1, on_vector)
+        quantize_w1(1, 1, on_vector)
+        message(0, 0, 256)
+        message(0, 256, 512)
+        gather(1, 3, 512, 1024)
+        weave(1, 512, 1024, on_vector)
+        message(1, 0, 256, False)
+        message(1, 256, 512, True)
+        update(0, 512)
+        message(0, 512, 768, False)
+        message(1, 512, 768, False)
+        update(512, 768)
+        message(0, 768, 1024, False)
+        message(1, 768, 896, False)
+        update(768, 896)
+        message(1, 896, 1024, False)
+        update(896, 1024)

@@ -1,6 +1,7 @@
 from contextlib import ExitStack
 
 import concourse.mybir as mybir
+from concourse.masks import make_identity
 
 K, T, S, H, N = 1024, 2048, 1024, 1024, 512
 FLOPS = 2 * K * H * S + 2 * H * N * S
@@ -56,9 +57,10 @@ def tile_list_relation_edge_messages_kernel(tc, xT, wgt, offs, w1, b1, gain, w2_
         w2_plane = keep.tile([P, 2, N], U8, name="w2_plane", align_bytes=64)
         nc.gpsimd.memset(w2_plane[:].rearrange("p a c -> p (a c)").bitcast(I32), 0)
 
-        nc.sync.dma_start(gains[:], gain.rearrange("(b p t) -> p b t", b=2, t=PACK))
-        nc.sync.dma_start(bias[:], b1.rearrange("(b p t) -> p b t", b=2, t=PACK))
-        nc.sync.dma_start(weights[:], wgt)
+        nc.scalar.dma_start(gains[:], gain.rearrange("(b p t) -> p b t", b=2, t=PACK))
+        nc.scalar.dma_start(bias[:], b1.rearrange("(b p t) -> p b t", b=2, t=PACK))
+        folded = keep.tile([P, P], F32, name="folded")
+        nc.sync.dma_start(folded[:], wgt.rearrange("(g r) (h c) -> g (r h) c", g=8, c=P)[:, :16, :])
         for i in range(PACK):
             load_x(0, i)
         load_x(1, 0)
@@ -82,6 +84,21 @@ def tile_list_relation_edge_messages_kernel(tc, xT, wgt, offs, w1, b1, gain, w2_
             old.append(keep.tile([P, N // P, BANK], F32, name=f"old_{h}", tag=f"slot_0_{h}", align_bytes=64))
             nc.sync.dma_start(old[h][:], e_rows[:, :, h * BANK : (h + 1) * BANK])
 
+        identity = keep.tile([P, P], F32, name="identity")
+        make_identity(nc, identity[:])
+        turned = psum.tile([P, P], F32, name="turned", tag="acc", bufs=5)
+        nc.tensor.transpose(turned[:], folded[:], identity[:])
+        by_block = turned[:].rearrange("c (g q) -> c q g", g=8)
+        for half in range(2):
+            spread = keep.tile([P, PACK, 8, 16], F32, name=f"spread_{half}")
+            nc.scalar.copy(
+                spread[:], by_block[:, PACK * half : PACK * (half + 1), :].unsqueeze(3).to_broadcast([P, PACK, 8, 16])
+            )
+            back = psum.tile([P, PACK, P], F32, name="back", tag="acc", bufs=5)
+            for h in range(PACK):
+                nc.tensor.transpose(back[:, h, :], spread[:, h, :, :].rearrange("c g r -> c (g r)"), identity[:])
+            nc.scalar.copy(weights[:, half * BANK : (half + 1) * BANK], back[:].rearrange("p h c -> p (h c)"))
+
         flat_gain = gains[:].rearrange("p b t -> p (b t)")
         size = keep.tile([P, 8], F32, name="size")
         nc.vector.scalar_tensor_tensor(size[:], flat_gain, -1.0, flat_gain, ALU.mult, ALU.max)
@@ -99,10 +116,12 @@ def tile_list_relation_edge_messages_kernel(tc, xT, wgt, offs, w1, b1, gain, w2_
         nc.vector.tensor_scalar_mul(root[:], twice[:], 0.5)
         root_bias = keep.tile([P, 8], F32, name="root_bias")
         nc.vector.tensor_tensor(root_bias[:], root[:], bias[:].rearrange("p b t -> p (b t)"), ALU.mult)
+        sign = keep.tile([P, 2, PACK], F32, name="sign")
+        nc.scalar.activation(sign[:], gains[:], ACT.Sign)
         signs = []
         for b in range(2):
             signs.append(keep.tile([P, SIGN_WIDTH, PACK], BF16, name=f"signs_{b}"))
-            nc.scalar.activation(signs[b][:], gains[:, b, :].unsqueeze(1).to_broadcast([P, SIGN_WIDTH, PACK]), ACT.Sign)
+            nc.vector.tensor_copy(signs[b][:], sign[:, b, :].unsqueeze(1).to_broadcast([P, SIGN_WIDTH, PACK]))
 
         x_codes = {}
         x_scales = [keep.tile([P, S], U8, name=f"x_scales_{a}", align_bytes=64) for a in range(2)]
@@ -110,14 +129,11 @@ def tile_list_relation_edge_messages_kernel(tc, xT, wgt, offs, w1, b1, gain, w2_
         m_scales = [keep.tile([P, S], U8, name=f"m_scales_{b}", align_bytes=64) for b in range(2)]
         w1_codes, w1_scales = {}, {}
 
-        picked = {}
+        picked = [keep.tile([P, PACK * S], F32, name=f"picked_{a}", align_bytes=64) for a in range(2)]
 
         def gather(a, i, j0, j1):
-            width = j1 - j0
-            if i == 0:
-                picked[a, j0] = keep.tile([P, PACK * width], F32, name=f"picked_{a}_{j0}", align_bytes=64)
             nc.vector.tensor_tensor(
-                picked[a, j0][:, i * width : (i + 1) * width],
+                picked[a][:, i * S + j0 : i * S + j1],
                 planes[a, i][:].indirect(offsets[:, j0 // 16 : j1 // 16]),
                 weights[:, j0:j1],
                 ALU.mult,
@@ -132,7 +148,7 @@ def tile_list_relation_edge_messages_kernel(tc, xT, wgt, offs, w1, b1, gain, w2_
                 woven = ring.tile([P, (j1 - j0) * PACK], BF16, name="woven", tag="woven", bufs=2, align_bytes=64)[:]
             copy(
                 woven.rearrange("p (c e i) -> p c i e", e=4, i=PACK),
-                picked[a, j0][:].rearrange("p (i c e) -> p c i e", e=4, i=PACK),
+                picked[a][:].rearrange("p (i j) -> p i j", i=PACK)[:, :, j0:j1].rearrange("p i (c e) -> p c i e", e=4),
             )
             nc.vector.quantize_mx(x_words(a, j0, j1), x_scales[a][:, j0:j1], woven)
 
@@ -185,10 +201,10 @@ def tile_list_relation_edge_messages_kernel(tc, xT, wgt, offs, w1, b1, gain, w2_
             )
             nc.vector.quantize_mx(m_codes[b][:, j0:j1].bitcast(FP8X4), m_scales[b][:, j0:j1], signed[:])
 
-        def update(j0, j1):
+        def update(j0, j1, per_bank=None):
             width = j1 - j0
             step = BANK if width == BANK else P
-            per_bank = BANK // width
+            per_bank = per_bank or BANK // width
             h, e0 = divmod(j0, BANK)
             for n0 in range(0, N // P, per_bank):
                 total = psum.tile([P, per_bank, width], F32, name="total", tag="total", bufs=3)
@@ -209,13 +225,12 @@ def tile_list_relation_edge_messages_kernel(tc, xT, wgt, offs, w1, b1, gain, w2_
                 nc.sync.dma_start(out_rows[:, n0 : n0 + per_bank, j0:j1], result)
 
         on_scalar, on_vector = nc.scalar.copy, nc.vector.tensor_copy
-        for i in range(PACK):
-            for j0 in (0, BANK):
-                gather(0, i, j0, j0 + BANK)
-        late_chunks = ((0, 256), (256, 512), (512, 1024))
+        gather(0, 0, 0, BANK)
+        gather(0, 0, BANK, S)
+        for i in range(1, PACK):
+            gather(0, i, 0, S)
         for i in range(PACK - 1):
-            for j0, j1 in late_chunks:
-                gather(1, i, j0, j1)
+            gather(1, i, 0, S)
         for a in range(2):
             for h in range(2):
                 x_codes[a, h] = keep.tile([P, BANK], U32, name=f"x_codes_{a}_{h}", align_bytes=64)[:]
@@ -224,7 +239,7 @@ def tile_list_relation_edge_messages_kernel(tc, xT, wgt, offs, w1, b1, gain, w2_
         quantize_w1(0, 0, on_scalar)
         quantize_w1(1, 0, on_scalar)
         gather(1, 3, 0, 256)
-        weave(1, 0, 256, on_scalar, picked[1, 512][:, 3 * BANK :].bitcast(BF16))
+        weave(1, 0, 256, on_scalar, picked[1][:, 3 * S + BANK :].bitcast(BF16))
         gather(1, 3, 256, 512)
         weave(1, 256, 512, on_scalar)
         quantize_w1(0, 1, on_vector)
@@ -233,14 +248,13 @@ def tile_list_relation_edge_messages_kernel(tc, xT, wgt, offs, w1, b1, gain, w2_
         message(0, 256, 512)
         gather(1, 3, 512, 1024)
         weave(1, 512, 1024, on_vector)
-        message(1, 0, 256, False)
-        message(1, 256, 512, True)
-        update(0, 512)
-        message(0, 512, 768, False)
-        message(1, 512, 768, False)
-        update(512, 768)
-        message(0, 768, 1024, False)
-        message(1, 768, 896, False)
-        update(768, 896)
-        message(1, 896, 1024, False)
-        update(896, 1024)
+        message(1,0,256)
+        message(1,256,512,True)
+        message(0,512,1024)
+        update(0,512)
+        message(1,512,768)
+        message(1,768,896)
+        update(512,768)
+        message(1,896,1024)
+        update(768,896)
+        update(896,1024,2)

@@ -84,25 +84,10 @@ def tile_list_relation_edge_messages_kernel(tc, xT, wgt, offs, w1, b1, gain, w2_
             old.append(keep.tile([P, N // P, BANK], F32, name=f"old_{h}", tag=f"slot_0_{h}", align_bytes=64))
             nc.sync.dma_start(old[h][:], e_rows[:, :, h * BANK : (h + 1) * BANK])
 
-        identity = keep.tile([P, P], F32, name="identity")
-        make_identity(nc, identity[:])
-        turned = psum.tile([P, P], F32, name="turned", tag="acc", bufs=5)
-        nc.tensor.transpose(turned[:], folded[:], identity[:])
-        by_block = turned[:].rearrange("c (g q) -> c q g", g=8)
-        for half in range(2):
-            spread = keep.tile([P, PACK, 8, 16], F32, name=f"spread_{half}")
-            nc.scalar.copy(
-                spread[:], by_block[:, PACK * half : PACK * (half + 1), :].unsqueeze(3).to_broadcast([P, PACK, 8, 16])
-            )
-            back = psum.tile([P, PACK, P], F32, name="back", tag="acc", bufs=5)
-            for h in range(PACK):
-                nc.tensor.transpose(back[:, h, :], spread[:, h, :, :].rearrange("c g r -> c (g r)"), identity[:])
-            nc.scalar.copy(weights[:, half * BANK : (half + 1) * BANK], back[:].rearrange("p h c -> p (h c)"))
-
         flat_gain = gains[:].rearrange("p b t -> p (b t)")
         size = keep.tile([P, 8], F32, name="size")
         nc.vector.scalar_tensor_tensor(size[:], flat_gain, -1.0, flat_gain, ALU.mult, ALU.max)
-        floored = keep.tile([P, 8], F32, name="floored")
+        floored = keep.tile([P, 8], F32, name="floored", tag="spread_0")
         nc.vector.tensor_scalar_max(floored[:], size[:], SQRT_FLOOR)
         guess = keep.tile([P, 8], F32, name="guess")
         nc.scalar.activation(guess[:], floored[:], ACT.Sqrt)
@@ -116,12 +101,29 @@ def tile_list_relation_edge_messages_kernel(tc, xT, wgt, offs, w1, b1, gain, w2_
         nc.vector.tensor_scalar_mul(root[:], twice[:], 0.5)
         root_bias = keep.tile([P, 8], F32, name="root_bias")
         nc.vector.tensor_tensor(root_bias[:], root[:], bias[:].rearrange("p b t -> p (b t)"), ALU.mult)
+        above = keep.tile([P, 2, PACK], F32, name="above")
+        nc.vector.tensor_single_scalar(above[:], gains[:], 0.0, ALU.is_gt)
         sign = keep.tile([P, 2, PACK], F32, name="sign")
-        nc.scalar.activation(sign[:], gains[:], ACT.Sign)
+        nc.vector.scalar_tensor_tensor(sign[:], gains[:], 0.0, above[:], ALU.is_ge, ALU.add)
         signs = []
         for b in range(2):
             signs.append(keep.tile([P, SIGN_WIDTH, PACK], BF16, name=f"signs_{b}"))
-            nc.vector.tensor_copy(signs[b][:], sign[:, b, :].unsqueeze(1).to_broadcast([P, SIGN_WIDTH, PACK]))
+            nc.vector.tensor_scalar_add(signs[b][:], sign[:, b, :].unsqueeze(1).to_broadcast([P, SIGN_WIDTH, PACK]), -1.0)
+
+        identity = keep.tile([P, P], F32, name="identity")
+        make_identity(nc, identity[:])
+        turned = psum.tile([P, P], F32, name="turned", tag="acc", bufs=5)
+        nc.tensor.transpose(turned[:], folded[:], identity[:])
+        by_block = turned[:].rearrange("c (g q) -> c q g", g=8)
+        for quarter in range(4):
+            spread = keep.tile([P, 2, 8, 16], F32, name=f"spread_{quarter}", tag=f"spread_{quarter}")
+            nc.scalar.copy(
+                spread[:], by_block[:, 2 * quarter : 2 * quarter + 2, :].unsqueeze(3).to_broadcast([P, 2, 8, 16])
+            )
+            back = psum.tile([P, 2, P], F32, name="back", tag="acc", bufs=5)
+            for h in range(2):
+                nc.tensor.transpose(back[:, h, :], spread[:, h, :, :].rearrange("c g r -> c (g r)"), identity[:])
+            nc.scalar.copy(weights[:, quarter * 256 : (quarter + 1) * 256], back[:].rearrange("p h c -> p (h c)"))
 
         x_codes = {}
         x_scales = [keep.tile([P, S], U8, name=f"x_scales_{a}", align_bytes=64) for a in range(2)]
@@ -225,11 +227,13 @@ def tile_list_relation_edge_messages_kernel(tc, xT, wgt, offs, w1, b1, gain, w2_
                 nc.sync.dma_start(out_rows[:, n0 : n0 + per_bank, j0:j1], result)
 
         on_scalar, on_vector = nc.scalar.copy, nc.vector.tensor_copy
-        gather(0, 0, 0, BANK)
-        gather(0, 0, BANK, S)
+        gather(0, 0, 0, 256)
+        gather(0, 0, 256, 512)
+        gather(0, 0, 512, 768)
+        gather(0, 0, 768, S)
         for i in range(1, PACK):
             gather(0, i, 0, S)
-        for i in range(PACK - 1):
+        for i in range(2):
             gather(1, i, 0, S)
         for a in range(2):
             for h in range(2):
@@ -238,18 +242,20 @@ def tile_list_relation_edge_messages_kernel(tc, xT, wgt, offs, w1, b1, gain, w2_
         weave(0, BANK, S, on_scalar)
         quantize_w1(0, 0, on_scalar)
         quantize_w1(1, 0, on_scalar)
-        gather(1, 3, 0, 256)
-        weave(1, 0, 256, on_scalar, picked[1][:, 3 * S + BANK :].bitcast(BF16))
-        gather(1, 3, 256, 512)
-        weave(1, 256, 512, on_scalar)
-        quantize_w1(0, 1, on_vector)
-        quantize_w1(1, 1, on_vector)
-        message(0, 0, 256)
-        message(0, 256, 512)
-        gather(1, 3, 512, 1024)
-        weave(1, 512, 1024, on_vector)
-        message(1,0,256)
-        message(1,256,512,True)
+        gather(1,2,0,512)
+        gather(1,3,0,256)
+        weave(1,0,256,on_scalar,picked[1][:, 3*S+512 : 3*S+512 + BANK].bitcast(BF16))
+        gather(1,3,256,512)
+        weave(1,256,512,on_scalar,picked[1][:, 2*S+512 : 2*S+512 + BANK].bitcast(BF16))
+        message(0,0,256)
+        message(0,256,512)
+        quantize_w1(0,1,on_vector)
+        quantize_w1(1,1,on_vector)
+        gather(1,2,512,S)
+        gather(1,3,512,S)
+        weave(1,512,1024,on_vector)
+        message(1,0,256,True)
+        message(1,256,512)
         message(0,512,1024)
         update(0,512)
         message(1,512,768)

@@ -19,11 +19,16 @@ ACT = mybir.ActivationFunctionType
 
 P = 128
 PACK = 4
-KP = P * PACK
-BANK = 512
-SQRT_FLOOR = 2.0 ** -110
+PASS = P * PACK
+PASSES = 2
+GROUPS = 8
+GROUP = P // GROUPS
+RUN = 4
+HALF, QUARTER, EIGHTH = S // 2, S // 4, S // 8
+STAGE1_BANKS, STAGE2_BANKS = 5, 3
+SQRT_FLOOR = 2.0**-110
 
-SIGN_WIDTH = 256
+VECTOR_SQUARES_FIRST, VECTOR_SQUARES_SECOND = 256, 128
 
 
 def tile_list_relation_edge_messages_kernel(tc, xT, wgt, offs, w1, b1, gain, w2_words, w2_scales, eT, out):
@@ -33,234 +38,227 @@ def tile_list_relation_edge_messages_kernel(tc, xT, wgt, offs, w1, b1, gain, w2_
         ring = ctx.enter_context(tc.tile_pool(name="ring", bufs=2))
         psum = ctx.enter_context(tc.psum_pool(name="psum", bufs=1))
 
-        offsets = keep.tile([P, S // 16], U16, name="offsets")
-        nc.sync.dma_start(offsets[:], offs)
-        weights = keep.tile([P, S], F32, name="weights")
-
-        x_rows = xT.rearrange("(a p i) t -> a i p t", a=2, i=PACK)
+        x_rows = xT.rearrange("(a p i) t -> a i p t", a=PASSES, i=PACK)
         planes = {}
 
-        def load_x(a, i):
-            planes[a, i] = keep.tile([P, T], F32, name=f"x_{a}_{i}", tag=f"slot_{a}_{i}", align_bytes=64)
+        def load_plane(a, i):
+            planes[a, i] = keep.tile([P, T], F32, name=f"plane_{a}_{i}", tag=f"slot_{a}_{i}", align_bytes=64)
             nc.sync.dma_start(planes[a, i][:], x_rows[a, i])
 
-        w1_rows = w1.rearrange("(a p i) (b c) -> a b p i c", a=2, i=PACK, b=2)
+        w1_rows = w1.rearrange("(a p i) (b c) -> a b p i c", a=PASSES, i=PACK, b=PASSES)
         w1_raw = {}
 
         def load_w1(a, b):
-            w1_raw[a, b] = keep.tile([P, PACK, KP], F32, name=f"w1_raw_{a}_{b}")
+            w1_raw[a, b] = keep.tile([P, PACK, PASS], F32, name=f"w1_raw_{a}_{b}")
             nc.sync.dma_start(w1_raw[a, b][:], w1_rows[a, b])
 
-        bias = keep.tile([P, 2, PACK], F32, name="bias")
-        gains = keep.tile([P, 2, PACK], F32, name="gains")
-        w2_codes = keep.tile([P, 2, 2 * N], U8, name="w2_codes", align_bytes=64)
-        w2_plane = keep.tile([P, 2, N], U8, name="w2_plane", align_bytes=64)
-        nc.gpsimd.memset(w2_plane[:].rearrange("p a c -> p (a c)").bitcast(I32), 0)
+        w2_codes = keep.tile([P, PASSES, 2 * N], U8, name="w2_codes", align_bytes=64)
+        w2_scale_rows = keep.tile([P, PASSES, N], U8, name="w2_scale_rows", align_bytes=64)
+        nc.gpsimd.memset(w2_scale_rows[:].rearrange("p b c -> p (b c)").bitcast(I32), 0)
 
-        nc.scalar.dma_start(gains[:], gain.rearrange("(b p t) -> p b t", b=2, t=PACK))
-        nc.scalar.dma_start(bias[:], b1.rearrange("(b p t) -> p b t", b=2, t=PACK))
+        gains = keep.tile([P, PASSES, PACK], F32, name="gains")
+        nc.scalar.dma_start(gains[:], gain.rearrange("(b p t) -> p b t", b=PASSES, t=PACK))
         folded = keep.tile([P, P], F32, name="folded")
-        nc.sync.dma_start(folded[:], wgt.rearrange("(g r) (h c) -> g (r h) c", g=8, c=P)[:, :16, :])
-        for i in range(PACK):
-            load_x(0, i)
-        load_x(1, 0)
-        load_x(1, 1)
+        nc.scalar.dma_start(folded[:], wgt.rearrange("(g r) (h c) -> g (r h) c", g=GROUPS, c=P)[:, :GROUP, :])
+        bias = keep.tile([P, PASSES, PACK], F32, name="bias")
+        nc.scalar.dma_start(bias[:], b1.rearrange("(b p t) -> p b t", b=PASSES, t=PACK))
+
+        load_plane(0, 0)
+        offsets = keep.tile([P, S // GROUP], U16, name="offsets")
+        nc.sync.dma_start(offsets[:], offs)
+        for i in range(1, PACK):
+            load_plane(0, i)
+        load_plane(1, 0)
+        load_plane(1, 1)
         load_w1(0, 0)
-        load_x(1, 2)
+        load_plane(1, 2)
         load_w1(1, 0)
-        load_x(1, 3)
+        load_plane(1, 3)
         load_w1(0, 1)
         load_w1(1, 1)
-        nc.sync.dma_start(w2_codes[:].bitcast(I32), w2_words.rearrange("a p c -> p a c").bitcast(I32))
+        nc.sync.dma_start(w2_codes[:].bitcast(I32), w2_words.rearrange("b p c -> p b c").bitcast(I32))
         for q in range(4):
             nc.sync.dma_start(
-                w2_plane[32 * q : 32 * q + 4, :, :].bitcast(I32),
-                w2_scales[:, 4 * q : 4 * q + 4, :].rearrange("a r c -> r a c").bitcast(I32),
+                w2_scale_rows[32 * q : 32 * q + 4, :, :].bitcast(I32),
+                w2_scales[:, 4 * q : 4 * q + 4, :].rearrange("b r c -> r b c").bitcast(I32),
             )
         e_rows = eT.rearrange("(n p) j -> p n j", p=P)
         out_rows = out.rearrange("(n p) j -> p n j", p=P)
         old = []
         for h in range(2):
-            old.append(keep.tile([P, N // P, BANK], F32, name=f"old_{h}", tag=f"slot_0_{h}", align_bytes=64))
-            nc.sync.dma_start(old[h][:], e_rows[:, :, h * BANK : (h + 1) * BANK])
+            old.append(keep.tile([P, N // P, HALF], F32, name=f"old_{h}", tag=f"slot_0_{h}", align_bytes=64))
+            nc.sync.dma_start(old[h][:], e_rows[:, :, h * HALF : (h + 1) * HALF])
 
+        columns = PASSES * PACK
         flat_gain = gains[:].rearrange("p b t -> p (b t)")
-        size = keep.tile([P, 8], F32, name="size")
+        size = keep.tile([P, columns], F32, name="size")
         nc.vector.scalar_tensor_tensor(size[:], flat_gain, -1.0, flat_gain, ALU.mult, ALU.max)
-        floored = keep.tile([P, 8], F32, name="floored", tag="spread_0")
+        floored = keep.tile([P, columns], F32, name="floored", tag="spread_0")
         nc.vector.tensor_scalar_max(floored[:], size[:], SQRT_FLOOR)
-        guess = keep.tile([P, 8], F32, name="guess")
+        guess = keep.tile([P, columns], F32, name="guess")
         nc.scalar.activation(guess[:], floored[:], ACT.Sqrt)
-        inverse = keep.tile([P, 8], F32, name="inverse")
+        inverse = keep.tile([P, columns], F32, name="inverse")
         nc.vector.reciprocal(inverse[:], guess[:])
-        quotient = keep.tile([P, 8], F32, name="quotient")
+        quotient = keep.tile([P, columns], F32, name="quotient")
         nc.vector.tensor_tensor(quotient[:], size[:], inverse[:], ALU.mult)
-        twice = keep.tile([P, 8], F32, name="twice")
+        twice = keep.tile([P, columns], F32, name="twice")
         nc.vector.tensor_tensor(twice[:], quotient[:], guess[:], ALU.add)
-        root = keep.tile([P, 8], F32, name="root")
+        root = keep.tile([P, columns], F32, name="root")
         nc.vector.tensor_scalar_mul(root[:], twice[:], 0.5)
-        root_bias = keep.tile([P, 8], F32, name="root_bias")
+        root_bias = keep.tile([P, columns], F32, name="root_bias")
         nc.vector.tensor_tensor(root_bias[:], root[:], bias[:].rearrange("p b t -> p (b t)"), ALU.mult)
-        above = keep.tile([P, 2, PACK], F32, name="above")
+        above = keep.tile([P, PASSES, PACK], F32, name="above")
         nc.vector.tensor_single_scalar(above[:], gains[:], 0.0, ALU.is_gt)
-        sign = keep.tile([P, 2, PACK], F32, name="sign")
-        nc.vector.scalar_tensor_tensor(sign[:], gains[:], 0.0, above[:], ALU.is_ge, ALU.add)
+        sign_plus_one = keep.tile([P, PASSES, PACK], F32, name="sign_plus_one")
+        nc.vector.scalar_tensor_tensor(sign_plus_one[:], gains[:], 0.0, above[:], ALU.is_ge, ALU.add)
         signs = []
-        for b in range(2):
-            signs.append(keep.tile([P, SIGN_WIDTH, PACK], BF16, name=f"signs_{b}"))
-            nc.vector.tensor_scalar_add(signs[b][:], sign[:, b, :].unsqueeze(1).to_broadcast([P, SIGN_WIDTH, PACK]), -1.0)
+        for b in range(PASSES):
+            signs.append(keep.tile([P, QUARTER, PACK], BF16, name=f"signs_{b}"))
+            nc.vector.tensor_scalar_add(
+                signs[b][:], sign_plus_one[:, b, :].unsqueeze(1).to_broadcast([P, QUARTER, PACK]), -1.0
+            )
 
+        weights = keep.tile([P, S], F32, name="weights")
         identity = keep.tile([P, P], F32, name="identity")
         make_identity(nc, identity[:])
-        turned = psum.tile([P, P], F32, name="turned", tag="acc", bufs=5)
+        turned = psum.tile([P, P], F32, name="turned", tag="stage1", bufs=STAGE1_BANKS)
         nc.tensor.transpose(turned[:], folded[:], identity[:])
-        by_block = turned[:].rearrange("c (g q) -> c q g", g=8)
+        by_block = turned[:].rearrange("c (g q) -> c q g", g=GROUPS)
+        blocks = QUARTER // P
         for quarter in range(4):
-            spread = keep.tile([P, 2, 8, 16], F32, name=f"spread_{quarter}", tag=f"spread_{quarter}")
-            nc.scalar.copy(
-                spread[:], by_block[:, 2 * quarter : 2 * quarter + 2, :].unsqueeze(3).to_broadcast([P, 2, 8, 16])
-            )
-            back = psum.tile([P, 2, P], F32, name="back", tag="acc", bufs=5)
-            for h in range(2):
+            spread = keep.tile([P, blocks, GROUPS, GROUP], F32, name=f"spread_{quarter}", tag=f"spread_{quarter}")
+            mine = by_block[:, blocks * quarter : blocks * (quarter + 1), :]
+            nc.scalar.copy(spread[:], mine.unsqueeze(3).to_broadcast([P, blocks, GROUPS, GROUP]))
+            back = psum.tile([P, blocks, P], F32, name="back", tag="stage1", bufs=STAGE1_BANKS)
+            for h in range(blocks):
                 nc.tensor.transpose(back[:, h, :], spread[:, h, :, :].rearrange("c g r -> c (g r)"), identity[:])
-            nc.scalar.copy(weights[:, quarter * 256 : (quarter + 1) * 256], back[:].rearrange("p h c -> p (h c)"))
+            nc.scalar.copy(weights[:, quarter * QUARTER : (quarter + 1) * QUARTER], back[:].rearrange("p h c -> p (h c)"))
 
-        x_codes = {}
-        x_scales = [keep.tile([P, S], U8, name=f"x_scales_{a}", align_bytes=64) for a in range(2)]
-        m_codes = [keep.tile([P, S], U32, name=f"m_codes_{b}", align_bytes=64) for b in range(2)]
-        m_scales = [keep.tile([P, S], U8, name=f"m_scales_{b}", align_bytes=64) for b in range(2)]
+        picked = [keep.tile([P, PACK * S], F32, name=f"picked_{a}", align_bytes=64) for a in range(PASSES)]
+        x_codes = [keep.tile([P, S], U32, name=f"x_codes_{a}", align_bytes=64) for a in range(PASSES)]
+        x_scales = [keep.tile([P, S], U8, name=f"x_scales_{a}", align_bytes=64) for a in range(PASSES)]
+        m_codes = [keep.tile([P, S], U32, name=f"m_codes_{b}", align_bytes=64) for b in range(PASSES)]
+        m_scales = [keep.tile([P, S], U8, name=f"m_scales_{b}", align_bytes=64) for b in range(PASSES)]
         w1_codes, w1_scales = {}, {}
-
-        picked = [keep.tile([P, PACK * S], F32, name=f"picked_{a}", align_bytes=64) for a in range(2)]
 
         def gather(a, i, j0, j1):
             nc.vector.tensor_tensor(
                 picked[a][:, i * S + j0 : i * S + j1],
-                planes[a, i][:].indirect(offsets[:, j0 // 16 : j1 // 16]),
+                planes[a, i][:].indirect(offsets[:, j0 // GROUP : j1 // GROUP]),
                 weights[:, j0:j1],
                 ALU.mult,
             )
 
-        def x_words(a, j0, j1):
-            h, c0 = divmod(j0, BANK)
-            return x_codes[a, h][:, c0 : c0 + j1 - j0].bitcast(FP8X4)
+        def woven_tile(width):
+            return ring.tile([P, width * PACK], BF16, name="woven", tag="woven", align_bytes=64)[:]
 
-        def weave(a, j0, j1, copy, woven=None):
-            if woven is None:
-                woven = ring.tile([P, (j1 - j0) * PACK], BF16, name="woven", tag="woven", bufs=2, align_bytes=64)[:]
+        def quantize_x(a, j0, j1, copy, woven):
             copy(
-                woven.rearrange("p (c e i) -> p c i e", e=4, i=PACK),
-                picked[a][:].rearrange("p (i j) -> p i j", i=PACK)[:, :, j0:j1].rearrange("p i (c e) -> p c i e", e=4),
+                woven.rearrange("p (c e i) -> p c i e", e=RUN, i=PACK),
+                picked[a][:].rearrange("p (i j) -> p i j", i=PACK)[:, :, j0:j1].rearrange("p i (c e) -> p c i e", e=RUN),
             )
-            nc.vector.quantize_mx(x_words(a, j0, j1), x_scales[a][:, j0:j1], woven)
+            nc.vector.quantize_mx(x_codes[a][:, j0:j1].bitcast(FP8X4), x_scales[a][:, j0:j1], woven)
 
-        def quantize_w1(a, b, copy, codes=None):
-            grouped = ring.tile([P, PACK, P, PACK], BF16, name="grouped", tag="grouped", bufs=2, align_bytes=64)
-            copy(
-                grouped[:].rearrange("p t m i -> p m i t"), w1_raw[a, b][:].rearrange("p i (m t) -> p m i t", t=PACK)
-            )
-            if codes is None:
-                codes = keep.tile([P, KP], U32, name=f"w1_codes_{a}_{b}", align_bytes=64)[:]
-            w1_codes[a, b] = codes
-            w1_scales[a, b] = keep.tile([P, KP], U8, name=f"w1_scales_{a}_{b}", align_bytes=64)
+        def quantize_w1(a, b, copy):
+            grouped = ring.tile([P, PACK, P, PACK], BF16, name="grouped", tag="grouped", align_bytes=64)
+            copy(grouped[:].rearrange("p t q i -> p q i t"), w1_raw[a, b][:].rearrange("p i (q t) -> p q i t", t=PACK))
+            w1_codes[a, b] = keep.tile([P, PASS], U32, name=f"w1_codes_{a}_{b}", align_bytes=64)
+            w1_scales[a, b] = keep.tile([P, PASS], U8, name=f"w1_scales_{a}_{b}", align_bytes=64)
             nc.vector.quantize_mx(
-                codes.bitcast(FP8X4), w1_scales[a, b][:], grouped[:].rearrange("p t m i -> p (t m i)")
+                w1_codes[a, b][:].bitcast(FP8X4), w1_scales[a, b][:], grouped[:].rearrange("p t q i -> p (t q i)")
             )
 
-        def message(b, j0, j1, square_on_vector=False):
+        def message(b, j0, j1, vector_squares=0):
             width = j1 - j0
-            rect = ring.tile([P, PACK, width], F32, name="rect", tag="rect", bufs=3)
+            rectified = ring.tile([P, PACK, width], F32, name="rectified", tag="rectified", bufs=3)
             for t in range(PACK):
-                acc = psum.tile([P, BANK], F32, name="acc", tag="acc", bufs=5)
-                for a in range(2):
+                acc = psum.tile([P, HALF], F32, name="acc", tag="stage1", bufs=STAGE1_BANKS)
+                for a in range(PASSES):
                     nc.tensor.matmul_mx(
                         acc[:, :width],
                         lhsT=w1_codes[a, b][:, t * P : (t + 1) * P].bitcast(FP8X4),
                         lhsT_scale=w1_scales[a, b][:, t * P : (t + 1) * P],
-                        rhs=x_words(a, j0, j1),
+                        rhs=x_codes[a][:, j0:j1].bitcast(FP8X4),
                         rhs_scale=x_scales[a][:, j0:j1],
                         start=(a == 0),
-                        stop=(a == 1),
+                        stop=(a == PASSES - 1),
                     )
-                col = PACK * b + t
+                col = slice(PACK * b + t, PACK * b + t + 1)
                 nc.scalar.activation(
-                    rect[:, t, :], acc[:, :width], ACT.Relu, bias=root_bias[:, col : col + 1], scale=root[:, col : col + 1]
+                    rectified[:, t, :], acc[:, :width], ACT.Relu, bias=root_bias[:, col], scale=root[:, col]
                 )
             squared = ring.tile([P, width, PACK], BF16, name="squared", tag="squared", bufs=3, align_bytes=64)
-            woven_out = squared[:].rearrange("p (c e) t -> p c t e", e=4)
-            woven_in = rect[:].rearrange("p t (c e) -> p c t e", e=4)
-            if square_on_vector:
-                nc.vector.tensor_tensor(woven_out, woven_in, woven_in, ALU.mult)
-            else:
-                nc.scalar.activation(woven_out, woven_in, ACT.Square)
-            signed = ring.tile([P, width * PACK], BF16, name="signed", tag="signed", bufs=2, align_bytes=64)
-            run = min(width, SIGN_WIDTH)
+            target = squared[:].rearrange("p (c e) t -> p c t e", e=RUN)
+            source = rectified[:].rearrange("p t (c e) -> p c t e", e=RUN)
+            cut = vector_squares // RUN
+            if cut:
+                nc.vector.tensor_tensor(target[:, :cut], source[:, :cut], source[:, :cut], ALU.mult)
+            nc.scalar.activation(target[:, cut:], source[:, cut:], ACT.Square)
+            signed = ring.tile([P, width * PACK], BF16, name="signed", tag="signed", align_bytes=64)
+            span = min(width, QUARTER)
+            pattern = signs[b][:, :span, :].rearrange("p j t -> p (j t)")
             nc.vector.tensor_tensor(
-                signed[:].rearrange("p (r e) -> p r e", e=run * PACK),
-                squared[:].rearrange("p (r j) t -> p r (j t)", j=run),
-                signs[b][:, :run, :].rearrange("p j t -> p (j t)").unsqueeze(1).to_broadcast([P, width // run, run * PACK]),
+                signed[:].rearrange("p (u v) -> p u v", v=span * PACK),
+                squared[:].rearrange("p (u j) t -> p u (j t)", j=span),
+                pattern.unsqueeze(1).to_broadcast([P, width // span, span * PACK]),
                 ALU.mult,
             )
             nc.vector.quantize_mx(m_codes[b][:, j0:j1].bitcast(FP8X4), m_scales[b][:, j0:j1], signed[:])
 
-        def update(j0, j1, per_bank=None):
+        def update(j0, j1, per_bank):
             width = j1 - j0
-            step = BANK if width == BANK else P
-            per_bank = per_bank or BANK // width
-            h, e0 = divmod(j0, BANK)
+            moving = HALF if width == HALF else P
+            h, e0 = divmod(j0, HALF)
             for n0 in range(0, N // P, per_bank):
-                total = psum.tile([P, per_bank, width], F32, name="total", tag="total", bufs=3)
+                total = psum.tile([P, per_bank, width], F32, name="total", tag="stage2", bufs=STAGE2_BANKS)
                 for n in range(n0, n0 + per_bank):
-                    for c0 in range(0, width, step):
-                        for b in range(2):
+                    for c0 in range(0, width, moving):
+                        cols = slice(j0 + c0, j0 + c0 + moving)
+                        for b in range(PASSES):
                             nc.tensor.matmul_mx(
-                                total[:, n - n0, c0 : c0 + step],
+                                total[:, n - n0, c0 : c0 + moving],
                                 lhsT=w2_codes[:, b, 2 * P * n : 2 * P * (n + 1)].bitcast(FP4X4),
-                                lhsT_scale=w2_plane[:, b, P * n : P * (n + 1)],
-                                rhs=m_codes[b][:, j0 + c0 : j0 + c0 + step].bitcast(FP8X4),
-                                rhs_scale=m_scales[b][:, j0 + c0 : j0 + c0 + step],
+                                lhsT_scale=w2_scale_rows[:, b, P * n : P * (n + 1)],
+                                rhs=m_codes[b][:, cols].bitcast(FP8X4),
+                                rhs_scale=m_scales[b][:, cols],
                                 start=(b == 0),
-                                stop=(b == 1),
+                                stop=(b == PASSES - 1),
                             )
                 result = old[h][:, n0 : n0 + per_bank, e0 : e0 + width]
                 nc.vector.tensor_tensor(result, total[:], result, ALU.add)
                 nc.sync.dma_start(out_rows[:, n0 : n0 + per_bank, j0:j1], result)
 
         on_scalar, on_vector = nc.scalar.copy, nc.vector.tensor_copy
-        gather(0, 0, 0, 256)
-        gather(0, 0, 256, 512)
-        gather(0, 0, 512, 768)
-        gather(0, 0, 768, S)
+        last = PACK - 1
+        for j0 in range(0, S, QUARTER):
+            gather(0, 0, j0, j0 + QUARTER)
         for i in range(1, PACK):
             gather(0, i, 0, S)
-        for i in range(2):
+        for i in range(last):
             gather(1, i, 0, S)
-        for a in range(2):
-            for h in range(2):
-                x_codes[a, h] = keep.tile([P, BANK], U32, name=f"x_codes_{a}_{h}", align_bytes=64)[:]
-        weave(0, 0, BANK, on_scalar)
-        weave(0, BANK, S, on_scalar)
-        quantize_w1(0, 0, on_scalar)
-        quantize_w1(1, 0, on_scalar)
-        gather(1,2,0,512)
-        gather(1,3,0,256)
-        weave(1,0,256,on_scalar,picked[1][:, 3*S+512 : 3*S+512 + BANK].bitcast(BF16))
-        gather(1,3,256,512)
-        weave(1,256,512,on_scalar,picked[1][:, 2*S+512 : 2*S+512 + BANK].bitcast(BF16))
-        message(0,0,256)
-        message(0,256,512)
-        quantize_w1(0,1,on_vector)
-        quantize_w1(1,1,on_vector)
-        gather(1,2,512,S)
-        gather(1,3,512,S)
-        weave(1,512,1024,on_vector)
-        message(1,0,256,True)
-        message(1,256,512)
-        message(0,512,1024)
-        update(0,512)
-        message(1,512,768)
-        message(1,768,896)
-        update(512,768)
-        message(1,896,1024)
-        update(768,896)
-        update(896,1024,2)
+        for j0 in (0, HALF):
+            quantize_x(0, j0, j0 + HALF, on_scalar, woven_tile(HALF))
+        for a in range(PASSES):
+            quantize_w1(a, 0, on_scalar)
+
+        gather(1, last, 0, QUARTER)
+        quantize_x(1, 0, QUARTER, on_scalar, picked[1][:, last * S + HALF :].bitcast(BF16))
+        gather(1, last, QUARTER, HALF)
+        quantize_x(1, QUARTER, HALF, on_scalar, woven_tile(QUARTER))
+        message(0, 0, QUARTER)
+        message(0, QUARTER, HALF)
+
+        for a in range(PASSES):
+            quantize_w1(a, 1, on_vector)
+        gather(1, last, HALF, S)
+        quantize_x(1, HALF, S, on_vector, woven_tile(HALF))
+        message(1, 0, HALF, VECTOR_SQUARES_FIRST)
+        message(0, HALF, S, VECTOR_SQUARES_SECOND)
+
+        update(0, HALF, 1)
+        message(1, HALF, S - QUARTER)
+        message(1, S - QUARTER, S - EIGHTH)
+        update(HALF, S - QUARTER, 2)
+        message(1, S - EIGHTH, S)
+        update(S - QUARTER, S - EIGHTH, 4)
+        update(S - EIGHTH, S, 2)

@@ -1,4 +1,5 @@
 from contextlib import ExitStack
+from itertools import product
 
 import concourse.mybir as mybir
 from concourse.masks import make_identity
@@ -58,15 +59,13 @@ def tile_list_relation_edge_messages_kernel(tc, xT, wgt, offs, w1, b1, gain, w2_
 
         gains = keep.tile([P, PASSES, PACK], F32, name="gains")
         nc.scalar.dma_start(gains[:], gain.rearrange("(b p t) -> p b t", b=PASSES, t=PACK))
-        folded = keep.tile([P, P], F32, name="folded")
-        nc.scalar.dma_start(folded[:], wgt.rearrange("(g r) (h c) -> g (r h) c", g=GROUPS, c=P)[:, :GROUP, :])
         bias = keep.tile([P, PASSES, PACK], F32, name="bias")
         nc.scalar.dma_start(bias[:], b1.rearrange("(b p t) -> p b t", b=PASSES, t=PACK))
-
-        load_plane(0, 0)
+        folded = keep.tile([P, P], F32, name="folded")
+        nc.sync.dma_start(folded[:], wgt.rearrange("(g r) (h c) -> g (r h) c", g=GROUPS, c=P)[:, :GROUP, :])
         offsets = keep.tile([P, S // GROUP], U16, name="offsets")
         nc.sync.dma_start(offsets[:], offs)
-        for i in range(1, PACK):
+        for i in range(PACK):
             load_plane(0, i)
         load_plane(1, 0)
         load_plane(1, 1)
@@ -100,23 +99,17 @@ def tile_list_relation_edge_messages_kernel(tc, xT, wgt, offs, w1, b1, gain, w2_
         inverse = keep.tile([P, columns], F32, name="inverse")
         nc.vector.reciprocal(inverse[:], guess[:])
         quotient = keep.tile([P, columns], F32, name="quotient")
-        nc.vector.tensor_tensor(quotient[:], size[:], inverse[:], ALU.mult)
+        nc.gpsimd.tensor_tensor(quotient[:], size[:], inverse[:], ALU.mult)
         twice = keep.tile([P, columns], F32, name="twice")
-        nc.vector.tensor_tensor(twice[:], quotient[:], guess[:], ALU.add)
+        nc.gpsimd.tensor_tensor(twice[:], quotient[:], guess[:], ALU.add)
         root = keep.tile([P, columns], F32, name="root")
-        nc.vector.tensor_scalar_mul(root[:], twice[:], 0.5)
+        nc.gpsimd.tensor_scalar_mul(root[:], twice[:], 0.5)
         root_bias = keep.tile([P, columns], F32, name="root_bias")
-        nc.vector.tensor_tensor(root_bias[:], root[:], bias[:].rearrange("p b t -> p (b t)"), ALU.mult)
+        nc.gpsimd.tensor_tensor(root_bias[:], root[:], bias[:].rearrange("p b t -> p (b t)"), ALU.mult)
         above = keep.tile([P, PASSES, PACK], F32, name="above")
         nc.vector.tensor_single_scalar(above[:], gains[:], 0.0, ALU.is_gt)
         sign_plus_one = keep.tile([P, PASSES, PACK], F32, name="sign_plus_one")
         nc.vector.scalar_tensor_tensor(sign_plus_one[:], gains[:], 0.0, above[:], ALU.is_ge, ALU.add)
-        signs = []
-        for b in range(PASSES):
-            signs.append(keep.tile([P, QUARTER, PACK], BF16, name=f"signs_{b}"))
-            nc.vector.tensor_scalar_add(
-                signs[b][:], sign_plus_one[:, b, :].unsqueeze(1).to_broadcast([P, QUARTER, PACK]), -1.0
-            )
 
         weights = keep.tile([P, S], F32, name="weights")
         identity = keep.tile([P, P], F32, name="identity")
@@ -133,6 +126,12 @@ def tile_list_relation_edge_messages_kernel(tc, xT, wgt, offs, w1, b1, gain, w2_
             for h in range(blocks):
                 nc.tensor.transpose(back[:, h, :], spread[:, h, :, :].rearrange("c g r -> c (g r)"), identity[:])
             nc.scalar.copy(weights[:, quarter * QUARTER : (quarter + 1) * QUARTER], back[:].rearrange("p h c -> p (h c)"))
+
+        signs = []
+        for b in range(PASSES):
+            signs.append(keep.tile([P, QUARTER, PACK], BF16, name=f"signs_{b}", tag=f"spread_{2 + b}"))
+            repeated = sign_plus_one[:, b, :].unsqueeze(1).to_broadcast([P, QUARTER, PACK])
+            nc.scalar.activation(signs[b][:], repeated, ACT.Copy, bias=-1.0)
 
         picked = [keep.tile([P, PACK * S], F32, name=f"picked_{a}", align_bytes=64) for a in range(PASSES)]
         x_codes = [keep.tile([P, S], U32, name=f"x_codes_{a}", align_bytes=64) for a in range(PASSES)]
@@ -211,19 +210,18 @@ def tile_list_relation_edge_messages_kernel(tc, xT, wgt, offs, w1, b1, gain, w2_
             h, e0 = divmod(j0, HALF)
             for n0 in range(0, N // P, per_bank):
                 total = psum.tile([P, per_bank, width], F32, name="total", tag="stage2", bufs=STAGE2_BANKS)
-                for n in range(n0, n0 + per_bank):
-                    for c0 in range(0, width, moving):
-                        cols = slice(j0 + c0, j0 + c0 + moving)
-                        for b in range(PASSES):
-                            nc.tensor.matmul_mx(
-                                total[:, n - n0, c0 : c0 + moving],
-                                lhsT=w2_codes[:, b, 2 * P * n : 2 * P * (n + 1)].bitcast(FP4X4),
-                                lhsT_scale=w2_scale_rows[:, b, P * n : P * (n + 1)],
-                                rhs=m_codes[b][:, cols].bitcast(FP8X4),
-                                rhs_scale=m_scales[b][:, cols],
-                                start=(b == 0),
-                                stop=(b == PASSES - 1),
-                            )
+                passes = list(product(range(PASSES), range(n0, n0 + per_bank), range(0, width, moving)))
+                for number, (b, n, c0) in enumerate(passes):
+                    cols = slice(j0 + c0, j0 + c0 + moving)
+                    nc.tensor.matmul_mx(
+                        total[:, n - n0, c0 : c0 + moving],
+                        lhsT=w2_codes[:, b, 2 * P * n : 2 * P * (n + 1)].bitcast(FP4X4),
+                        lhsT_scale=w2_scale_rows[:, b, P * n : P * (n + 1)],
+                        rhs=m_codes[b][:, cols].bitcast(FP8X4),
+                        rhs_scale=m_scales[b][:, cols],
+                        start=(number == 0),
+                        stop=(number == len(passes) - 1),
+                    )
                 result = old[h][:, n0 : n0 + per_bank, e0 : e0 + width]
                 nc.vector.tensor_tensor(result, total[:], result, ALU.add)
                 nc.sync.dma_start(out_rows[:, n0 : n0 + per_bank, j0:j1], result)

from contextlib import ExitStack
from itertools import product

import concourse.mybir as mybir
from concourse.masks import make_identity

K, T, S, H, N = 1024, 2048, 1024, 1024, 512
FLOPS = 2 * K * H * S + 2 * H * N * S

F32 = mybir.dt.float32
BF16 = mybir.dt.bfloat16
I32 = mybir.dt.int32
U32 = mybir.dt.uint32
U16 = mybir.dt.uint16
U8 = mybir.dt.uint8
FP8X4 = mybir.dt.float8_e4m3fn_x4
FP4X4 = mybir.dt.float4_e2m1fn_x4
ALU = mybir.AluOpType
ACT = mybir.ActivationFunctionType

P = 128
PACK = 4
PASS = P * PACK
PASSES = 2
GROUPS = 8
GROUP = P // GROUPS
RUN = 4
HALF, QUARTER, EIGHTH = S // 2, S // 4, S // 8
STAGE1_BANKS, STAGE2_BANKS = 5, 3
SQRT_FLOOR = 2.0**-110

VECTOR_SQUARES_FIRST, VECTOR_SQUARES_SECOND = 256, 128


def tile_list_relation_edge_messages_kernel(tc, xT, wgt, offs, w1, b1, gain, w2_words, w2_scales, eT, out):
    nc = tc.nc
    with ExitStack() as ctx:
        keep = ctx.enter_context(tc.tile_pool(name="keep", bufs=1))
        ring = ctx.enter_context(tc.tile_pool(name="ring", bufs=2))
        psum = ctx.enter_context(tc.psum_pool(name="psum", bufs=1))

        x_rows = xT.rearrange("(a p i) t -> a i p t", a=PASSES, i=PACK)
        planes = {}

        def load_plane(a, i):
            planes[a, i] = keep.tile([P, T], F32, name=f"plane_{a}_{i}", tag=f"slot_{a}_{i}", align_bytes=64)
            nc.sync.dma_start(planes[a, i][:], x_rows[a, i])

        w1_rows = w1.rearrange("(a p i) (b c) -> a b p i c", a=PASSES, i=PACK, b=PASSES)
        w1_raw = {}

        def load_w1(a, b):
            w1_raw[a, b] = keep.tile([P, PACK, PASS], F32, name=f"w1_raw_{a}_{b}")
            nc.sync.dma_start(w1_raw[a, b][:], w1_rows[a, b])

        w2_codes = keep.tile([P, PASSES, 2 * N], U8, name="w2_codes", align_bytes=64)
        w2_scale_rows = keep.tile([P, PASSES, N], U8, name="w2_scale_rows", align_bytes=64)
        nc.gpsimd.memset(w2_scale_rows[:].rearrange("p b c -> p (b c)").bitcast(I32), 0)

        gains = keep.tile([P, PASSES, PACK], F32, name="gains")
        nc.scalar.dma_start(gains[:], gain.rearrange("(b p t) -> p b t", b=PASSES, t=PACK))
        bias = keep.tile([P, PASSES, PACK], F32, name="bias")
        nc.scalar.dma_start(bias[:], b1.rearrange("(b p t) -> p b t", b=PASSES, t=PACK))
        folded = keep.tile([P, P], F32, name="folded")
        nc.sync.dma_start(folded[:], wgt.rearrange("(g r) (h c) -> g (r h) c", g=GROUPS, c=P)[:, :GROUP, :])
        offsets = keep.tile([P, S // GROUP], U16, name="offsets")
        nc.sync.dma_start(offsets[:], offs)
        for i in range(PACK):
            load_plane(0, i)
        load_plane(1, 0)
        load_plane(1, 1)
        load_w1(0, 0)
        load_plane(1, 2)
        load_w1(1, 0)
        load_plane(1, 3)
        load_w1(0, 1)
        load_w1(1, 1)
        nc.sync.dma_start(w2_codes[:].bitcast(I32), w2_words.rearrange("b p c -> p b c").bitcast(I32))
        for q in range(4):
            nc.sync.dma_start(
                w2_scale_rows[32 * q : 32 * q + 4, :, :].bitcast(I32),
                w2_scales[:, 4 * q : 4 * q + 4, :].rearrange("b r c -> r b c").bitcast(I32),
            )
        e_rows = eT.rearrange("(n p) j -> p n j", p=P)
        out_rows = out.rearrange("(n p) j -> p n j", p=P)
        old = []
        for h in range(2):
            old.append(keep.tile([P, N // P, HALF], F32, name=f"old_{h}", tag=f"slot_0_{h}", align_bytes=64))
            nc.sync.dma_start(old[h][:], e_rows[:, :, h * HALF : (h + 1) * HALF])

        columns = PASSES * PACK
        flat_gain = gains[:].rearrange("p b t -> p (b t)")
        size = keep.tile([P, columns], F32, name="size")
        nc.vector.scalar_tensor_tensor(size[:], flat_gain, -1.0, flat_gain, ALU.mult, ALU.max)
        floored = keep.tile([P, columns], F32, name="floored", tag="spread_0")
        nc.vector.tensor_scalar_max(floored[:], size[:], SQRT_FLOOR)
        guess = keep.tile([P, columns], F32, name="guess")
        nc.scalar.activation(guess[:], floored[:], ACT.Sqrt)
        inverse = keep.tile([P, columns], F32, name="inverse")
        nc.vector.reciprocal(inverse[:], guess[:])
        quotient = keep.tile([P, columns], F32, name="quotient")
        nc.gpsimd.tensor_tensor(quotient[:], size[:], inverse[:], ALU.mult)
        twice = keep.tile([P, columns], F32, name="twice")
        nc.gpsimd.tensor_tensor(twice[:], quotient[:], guess[:], ALU.add)
        root = keep.tile([P, columns], F32, name="root")
        nc.gpsimd.tensor_scalar_mul(root[:], twice[:], 0.5)
        root_bias = keep.tile([P, columns], F32, name="root_bias")
        nc.gpsimd.tensor_tensor(root_bias[:], root[:], bias[:].rearrange("p b t -> p (b t)"), ALU.mult)
        above = keep.tile([P, PASSES, PACK], F32, name="above")
        nc.vector.tensor_single_scalar(above[:], gains[:], 0.0, ALU.is_gt)
        sign_plus_one = keep.tile([P, PASSES, PACK], F32, name="sign_plus_one")
        nc.vector.scalar_tensor_tensor(sign_plus_one[:], gains[:], 0.0, above[:], ALU.is_ge, ALU.add)

        weights = keep.tile([P, S], F32, name="weights")
        identity = keep.tile([P, P], F32, name="identity")
        make_identity(nc, identity[:])
        turned = psum.tile([P, P], F32, name="turned", tag="stage1", bufs=STAGE1_BANKS)
        nc.tensor.transpose(turned[:], folded[:], identity[:])
        by_block = turned[:].rearrange("c (g q) -> c q g", g=GROUPS)
        blocks = QUARTER // P
        for quarter in range(4):
            spread = keep.tile([P, blocks, GROUPS, GROUP], F32, name=f"spread_{quarter}", tag=f"spread_{quarter}")
            mine = by_block[:, blocks * quarter : blocks * (quarter + 1), :]
            nc.scalar.copy(spread[:], mine.unsqueeze(3).to_broadcast([P, blocks, GROUPS, GROUP]))
            back = psum.tile([P, blocks, P], F32, name="back", tag="stage1", bufs=STAGE1_BANKS)
            for h in range(blocks):
                nc.tensor.transpose(back[:, h, :], spread[:, h, :, :].rearrange("c g r -> c (g r)"), identity[:])
            nc.scalar.copy(weights[:, quarter * QUARTER : (quarter + 1) * QUARTER], back[:].rearrange("p h c -> p (h c)"))

        signs = []
        for b in range(PASSES):
            signs.append(keep.tile([P, QUARTER, PACK], BF16, name=f"signs_{b}", tag=f"spread_{2 + b}"))
            repeated = sign_plus_one[:, b, :].unsqueeze(1).to_broadcast([P, QUARTER, PACK])
            nc.scalar.activation(signs[b][:], repeated, ACT.Copy, bias=-1.0)

        picked = [keep.tile([P, PACK * S], F32, name=f"picked_{a}", align_bytes=64) for a in range(PASSES)]
        x_codes = [keep.tile([P, S], U32, name=f"x_codes_{a}", align_bytes=64) for a in range(PASSES)]
        x_scales = [keep.tile([P, S], U8, name=f"x_scales_{a}", align_bytes=64) for a in range(PASSES)]
        m_codes = [keep.tile([P, S], U32, name=f"m_codes_{b}", align_bytes=64) for b in range(PASSES)]
        m_scales = [keep.tile([P, S], U8, name=f"m_scales_{b}", align_bytes=64) for b in range(PASSES)]
        w1_codes, w1_scales = {}, {}

        def gather(a, i, j0, j1):
            nc.vector.tensor_tensor(
                picked[a][:, i * S + j0 : i * S + j1],
                planes[a, i][:].indirect(offsets[:, j0 // GROUP : j1 // GROUP]),
                weights[:, j0:j1],
                ALU.mult,
            )

        def woven_tile(width):
            return ring.tile([P, width * PACK], BF16, name="woven", tag="woven", align_bytes=64)[:]

        def quantize_x(a, j0, j1, copy, woven):
            copy(
                woven.rearrange("p (c e i) -> p c i e", e=RUN, i=PACK),
                picked[a][:].rearrange("p (i j) -> p i j", i=PACK)[:, :, j0:j1].rearrange("p i (c e) -> p c i e", e=RUN),
            )
            nc.vector.quantize_mx(x_codes[a][:, j0:j1].bitcast(FP8X4), x_scales[a][:, j0:j1], woven)

        def quantize_w1(a, b, copy):
            grouped = ring.tile([P, PACK, P, PACK], BF16, name="grouped", tag="grouped", align_bytes=64)
            copy(grouped[:].rearrange("p t q i -> p q i t"), w1_raw[a, b][:].rearrange("p i (q t) -> p q i t", t=PACK))
            w1_codes[a, b] = keep.tile([P, PASS], U32, name=f"w1_codes_{a}_{b}", align_bytes=64)
            w1_scales[a, b] = keep.tile([P, PASS], U8, name=f"w1_scales_{a}_{b}", align_bytes=64)
            nc.vector.quantize_mx(
                w1_codes[a, b][:].bitcast(FP8X4), w1_scales[a, b][:], grouped[:].rearrange("p t q i -> p (t q i)")
            )

        def message(b, j0, j1, vector_squares=0):
            width = j1 - j0
            rectified = ring.tile([P, PACK, width], F32, name="rectified", tag="rectified", bufs=3)
            for t in range(PACK):
                acc = psum.tile([P, HALF], F32, name="acc", tag="stage1", bufs=STAGE1_BANKS)
                for a in range(PASSES):
                    nc.tensor.matmul_mx(
                        acc[:, :width],
                        lhsT=w1_codes[a, b][:, t * P : (t + 1) * P].bitcast(FP8X4),
                        lhsT_scale=w1_scales[a, b][:, t * P : (t + 1) * P],
                        rhs=x_codes[a][:, j0:j1].bitcast(FP8X4),
                        rhs_scale=x_scales[a][:, j0:j1],
                        start=(a == 0),
                        stop=(a == PASSES - 1),
                    )
                col = slice(PACK * b + t, PACK * b + t + 1)
                nc.scalar.activation(
                    rectified[:, t, :], acc[:, :width], ACT.Relu, bias=root_bias[:, col], scale=root[:, col]
                )
            squared = ring.tile([P, width, PACK], BF16, name="squared", tag="squared", bufs=3, align_bytes=64)
            target = squared[:].rearrange("p (c e) t -> p c t e", e=RUN)
            source = rectified[:].rearrange("p t (c e) -> p c t e", e=RUN)
            cut = vector_squares // RUN
            if cut:
                nc.vector.tensor_tensor(target[:, :cut], source[:, :cut], source[:, :cut], ALU.mult)
            nc.scalar.activation(target[:, cut:], source[:, cut:], ACT.Square)
            signed = ring.tile([P, width * PACK], BF16, name="signed", tag="signed", align_bytes=64)
            span = min(width, QUARTER)
            pattern = signs[b][:, :span, :].rearrange("p j t -> p (j t)")
            nc.vector.tensor_tensor(
                signed[:].rearrange("p (u v) -> p u v", v=span * PACK),
                squared[:].rearrange("p (u j) t -> p u (j t)", j=span),
                pattern.unsqueeze(1).to_broadcast([P, width // span, span * PACK]),
                ALU.mult,
            )
            nc.vector.quantize_mx(m_codes[b][:, j0:j1].bitcast(FP8X4), m_scales[b][:, j0:j1], signed[:])

        def update(j0, j1, per_bank):
            width = j1 - j0
            moving = HALF if width == HALF else P
            h, e0 = divmod(j0, HALF)
            for n0 in range(0, N // P, per_bank):
                total = psum.tile([P, per_bank, width], F32, name="total", tag="stage2", bufs=STAGE2_BANKS)
                passes = list(product(range(PASSES), range(n0, n0 + per_bank), range(0, width, moving)))
                for number, (b, n, c0) in enumerate(passes):
                    cols = slice(j0 + c0, j0 + c0 + moving)
                    nc.tensor.matmul_mx(
                        total[:, n - n0, c0 : c0 + moving],
                        lhsT=w2_codes[:, b, 2 * P * n : 2 * P * (n + 1)].bitcast(FP4X4),
                        lhsT_scale=w2_scale_rows[:, b, P * n : P * (n + 1)],
                        rhs=m_codes[b][:, cols].bitcast(FP8X4),
                        rhs_scale=m_scales[b][:, cols],
                        start=(number == 0),
                        stop=(number == len(passes) - 1),
                    )
                result = old[h][:, n0 : n0 + per_bank, e0 : e0 + width]
                nc.vector.tensor_tensor(result, total[:], result, ALU.add)
                nc.sync.dma_start(out_rows[:, n0 : n0 + per_bank, j0:j1], result)

        on_scalar, on_vector = nc.scalar.copy, nc.vector.tensor_copy
        last = PACK - 1
        for j0 in range(0, S, QUARTER):
            gather(0, 0, j0, j0 + QUARTER)
        for i in range(1, PACK):
            gather(0, i, 0, S)
        for i in range(last):
            gather(1, i, 0, S)
        for j0 in (0, HALF):
            quantize_x(0, j0, j0 + HALF, on_scalar, woven_tile(HALF))
        for a in range(PASSES):
            quantize_w1(a, 0, on_scalar)

        gather(1, last, 0, QUARTER)
        quantize_x(1, 0, QUARTER, on_scalar, picked[1][:, last * S + HALF :].bitcast(BF16))
        gather(1, last, QUARTER, HALF)
        quantize_x(1, QUARTER, HALF, on_scalar, woven_tile(QUARTER))
        message(0, 0, QUARTER)
        message(0, QUARTER, HALF)

        for a in range(PASSES):
            quantize_w1(a, 1, on_vector)
        gather(1, last, HALF, S)
        quantize_x(1, HALF, S, on_vector, woven_tile(HALF))
        message(1, 0, HALF, VECTOR_SQUARES_FIRST)
        message(0, HALF, S, VECTOR_SQUARES_SECOND)

        update(0, HALF, 1)
        message(1, HALF, S - QUARTER)
        message(1, S - QUARTER, S - EIGHTH)
        update(HALF, S - QUARTER, 2)
        message(1, S - EIGHTH, S)
        update(S - QUARTER, S - EIGHTH, 4)
        update(S - EIGHTH, S, 2)
